import numpy as np
import ml_dtypes


def mxq(x, axis, fmt="e4m3"):
    dtype, down = {"e4m3": (ml_dtypes.float8_e4m3fn, 7), "e5m2": (ml_dtypes.float8_e5m2, 14)}[fmt]
    v = np.moveaxis(np.asarray(x, np.float32).astype(ml_dtypes.bfloat16).astype(np.float64), axis, -1)
    blocks = v.reshape(v.shape[:-1] + (-1, 32))
    amax = np.abs(blocks).max(-1, keepdims=True)
    byte = np.maximum(np.where(amax > 0, np.frexp(amax)[1] - 1 + 127, 0) - down, 1)
    scale = np.exp2(byte - 127.0)
    codes = (blocks / scale).astype(np.float32).astype(dtype).astype(np.float64)
    return np.moveaxis((codes * scale).reshape(v.shape), -1, axis)


WIDE = False


def mx_kscale(k):
    if not WIDE:
        return np.ones(k)
    levels = np.array([10, -10, 5, -5, 0])
    if k % 512:
        return np.exp2(np.random.permutation(np.resize(levels, k // 32))).repeat(32)
    a = np.empty((k // 512, 16))
    for p in range(k // 512):
        a[p, :8] = np.random.permutation(np.resize(levels, 8))
        for g in range(8):
            far = levels[np.abs(levels - a[p, g]) >= 10]
            a[p, g + 8] = far[np.random.randint(len(far))]
    return np.exp2(a.ravel()).repeat(32)


def f64(x):
    return np.asarray(x).astype(np.float64)


def striped(idx):
    return np.tile(idx.reshape(-1, 16).T, (8, 1)).astype(np.uint16)


def unstriped(offs):
    return offs[:16].T.reshape(-1).astype(np.int64)


def pack_weight(w):
    k, n = w.shape
    w = f64(np.asarray(w, np.float32).astype(ml_dtypes.bfloat16)).reshape(k // 32, 32, n)
    amax = np.abs(w).max(1)
    byte = np.clip(np.where(amax > 0, np.frexp(amax)[1] - 1 + 127 - 7, 1), 1, 254)
    scaled = (w * np.exp2(127.0 - byte)[:, None, :]).reshape(k, n).astype(np.float32)
    words = np.ascontiguousarray(scaled.reshape(k // 512, 128, 4, n).transpose(0, 1, 3, 2)).astype(ml_dtypes.float8_e4m3fn).view(np.uint8)
    return words, np.ascontiguousarray(byte.astype(np.uint8).reshape(k // 512, 16, n))


def unpack_weight(words, scales):
    g, p, n, _ = words.shape
    vals = np.ascontiguousarray(words).view(ml_dtypes.float8_e4m3fn).astype(np.float64) * np.repeat(np.exp2(scales.astype(np.float64) - 127.0), 8, axis=1)[..., None]
    return vals.transpose(0, 1, 3, 2).reshape(g * 512, n)


E2M1 = np.array([0.0, 0.5, 1.0, 1.5, 2.0, 3.0, 4.0, 6.0, -0.0, -0.5, -1.0, -1.5, -2.0, -3.0, -4.0, -6.0])


def pack_fp4(w):
    k, n = w.shape
    w = f64(np.asarray(w, np.float32).astype(ml_dtypes.bfloat16)).reshape(k // 32, 32, n)
    amax = np.abs(w).max(1)
    mant, ex = np.frexp(amax / 6.0)
    byte = np.clip(np.where(amax > 0, np.where(mant > 0.5, ex, ex - 1) + 127, 1), 1, 254)
    scaled = (w * np.exp2(127.0 - byte)[:, None, :]).reshape(k, n).astype(np.float32)
    c = np.ascontiguousarray(scaled.reshape(k // 512, 128, 4, n).transpose(0, 1, 3, 2)).astype(ml_dtypes.float4_e2m1fn).view(np.uint8) & 0xF
    words = (c[..., 0::2] | (c[..., 1::2] << 4)).reshape(k // 512, 128, 2 * n)
    return np.ascontiguousarray(words), np.ascontiguousarray(byte.astype(np.uint8).reshape(k // 512, 16, n))


def unpack_fp4(words, scales):
    g, _, n = scales.shape
    words = np.ascontiguousarray(words).reshape(g, 128, n, 2)
    nib = np.empty((g, 128, n, 4), np.uint8)
    nib[..., 0::2] = words & 0xF
    nib[..., 1::2] = words >> 4
    vals = E2M1[nib] * np.repeat(np.exp2(scales.astype(np.float64) - 127.0), 8, axis=1)[..., None]
    return vals.transpose(0, 1, 3, 2).reshape(g * 512, n)


def planes(y):
    n, m = y.shape
    v = y.astype(np.float32).astype(ml_dtypes.bfloat16).astype(np.float64).reshape(n // 32, 32, m)
    top = np.abs(v).max(1)
    byte = np.clip(np.where(top > 0, np.frexp(top)[1] - 1 + 127 - 7, 1), 1, 254)
    codes = (v * np.exp2(127.0 - byte)[:, None, :]).reshape(n, m).astype(np.float32).astype(ml_dtypes.float8_e4m3fn).view(np.uint8)
    words = codes.reshape(n // 512, 128, 4, m).transpose(0, 1, 3, 2)
    return np.ascontiguousarray(words), np.ascontiguousarray(byte.astype(np.uint8).reshape(n // 512, 16, m))


def relu(v):
    return np.maximum(v, 0.0)


K, T, S, D, V, H, N = 512, 1024, 512, 3, 256, 512, 512
P = 2 ** 7


def setup_inputs():
    n = np.random.standard_normal
    s = mx_kscale(K)[:, None]
    u = mx_kscale(H)
    near = np.random.permutation(S)
    packed_xT = pack_weight(n((K, T)) * s)
    packed_w2 = pack_fp4(n((H, N)) / np.sqrt(3 * H) / u[:, None])
    packed_w3 = pack_fp4(n((H, N)) / np.sqrt(3 * H) / u[:, None])
    packed_w4 = pack_fp4(n((H, N)) / np.sqrt(3 * H) / u[:, None])
    return {
        "x_words": packed_xT[0],
        "x_scales": packed_xT[1],
        "w1": (n((K, H)) / np.sqrt(K) / s * u).astype(np.float32),
        "w2_words": packed_w2[0],
        "w2_scales": packed_w2[1],
        "w3_words": packed_w3[0],
        "w3_scales": packed_w3[1],
        "w4_words": packed_w4[0],
        "w4_scales": packed_w4[1],
        "gate": (np.tile(np.random.uniform(0.2, 1.0, (D, 1, V)) / np.sqrt(D), (1, P, 1))).astype(np.float32),
        "gate2": (np.tile(np.random.uniform(0.2, 1.0, (D, 1, V)) / np.sqrt(D), (1, P, 1))).astype(np.float32),
        "offs": striped(np.random.permutation(T)[:S]),
        "cen": striped(np.random.permutation(S)[:V]),
        "pos1": striped(near[:V]),
        "pos2": striped(near[V:]),
        "pos3": striped(np.random.permutation(S)[:V]),
        "far1": striped(np.random.permutation(S)[:V]),
        "far2": striped(np.random.permutation(S)[:V]),
        "far3": striped(np.random.permutation(S)[:V]),
    }


def reference(x_words, x_scales, w1, w2_words, w2_scales, w3_words, w3_scales, w4_words, w4_scales, gate, gate2, offs, cen, pos1, pos2, pos3, far1, far2, far3):
    xq = unpack_weight(x_words, x_scales)[:, unstriped(offs)]
    h = relu(mxq(f64(w1), 0, "e4m3").T @ xq)
    z0 = h[:, unstriped(cen)]
    z1 = h[:, unstriped(pos1)] * f64(gate)[0, :1] + h[:, unstriped(pos2)] * f64(gate)[1, :1] + h[:, unstriped(pos3)] * f64(gate)[2, :1]
    z2 = h[:, unstriped(far1)] * f64(gate2)[0, :1] + h[:, unstriped(far2)] * f64(gate2)[1, :1] + h[:, unstriped(far3)] * f64(gate2)[2, :1]
    out_0 = unpack_fp4(w2_words, w2_scales).T @ mxq(z0, 0, "e4m3") + unpack_fp4(w3_words, w3_scales).T @ mxq(z1, 0, "e4m3") + unpack_fp4(w4_words, w4_scales).T @ mxq(z2, 0, "e4m3")
    return (out_0,) + planes(out_0)

@@ -1,0 +1,258 @@
+from contextlib import ExitStack
+
+import concourse.mybir as mybir
+from concourse.masks import make_identity
+
+K, T, S, D, V, H, N = 512, 1024, 512, 3, 256, 512, 512
+FLOPS = 2 * K * H * S + 3 * 2 * H * N * V
+
+F32 = mybir.dt.float32
+BF16 = mybir.dt.bfloat16
+I32 = mybir.dt.int32
+U32 = mybir.dt.uint32
+U16 = mybir.dt.uint16
+U8 = mybir.dt.uint8
+FP8X4 = mybir.dt.float8_e4m3fn_x4
+FP4X4 = mybir.dt.float4_e2m1fn_x4
+ACT = mybir.ActivationFunctionType
+ALU = mybir.AluOpType
+
+P = 128
+PACK = 4
+HALF = 128
+COLS = HALF // 16
+
+
+def tile_picked_zmix_none_po_kernel(
+    tc, x_words, x_scales, w1, w2_words, w2_scales, w3_words, w3_scales, w4_words, w4_scales,
+    gate, gate2, offs, cen, pos1, pos2, pos3, far1, far2, far3, out_0, out_1, out_2,
+):
+    nc = tc.nc
+    with ExitStack() as ctx:
+        keep = ctx.enter_context(tc.tile_pool(name="keep", bufs=1))
+        ring = ctx.enter_context(tc.tile_pool(name="ring", bufs=4))
+        acc = ctx.enter_context(tc.psum_pool(name="acc", bufs=1))
+        turn = ctx.enter_context(tc.psum_pool(name="turn", bufs=2))
+
+        def load_list(name, source):
+            tile = keep.tile(list(source.shape), U16, name=name)
+            nc.sync.dma_start(tile[:], source)
+            return tile
+
+        xs = keep.tile([P, T], U8, name="xs", align_bytes=64)
+        nc.vector.memset(xs[:].bitcast(I32), 0)
+        ws_raw = keep.tile([P, 3, N], U8, name="ws_raw", align_bytes=64)
+        nc.gpsimd.memset(ws_raw[:].rearrange("p w n -> p (w n)").bitcast(I32), 0)
+        ident = keep.tile([P, P], F32, name="ident")
+        make_identity(nc, ident[:])
+
+        offs_t = load_list("offs_t", offs)
+        near = [load_list("pos0_t", pos1)]
+        for q in range(4):
+            nc.scalar.dma_start(xs[32 * q : 32 * q + 4, :].bitcast(I32), x_scales[0, 4 * q : 4 * q + 4, :].bitcast(I32))
+        xw = keep.tile([P, T], U32, name="xw", align_bytes=64)
+        nc.sync.dma_start(xw[:].bitcast(I32), x_words[0].rearrange("p n t -> p (n t)").bitcast(I32))
+        w1_rows = w1.rearrange("(p j) c -> p j c", j=PACK)
+        w1_raw = []
+        for q in range(4):
+            part = keep.tile([P, PACK, P], F32, name="w1_raw%d" % q)
+            nc.sync.dma_start(part[:], w1_rows[:, :, q * P : (q + 1) * P])
+            w1_raw.append(part)
+        ww_raw = []
+        for w, source in enumerate((w3_words, w4_words, w2_words)):
+            part = keep.tile([P, 2 * N], U8, name="ww_raw%d" % w, align_bytes=64)
+            nc.sync.dma_start(part[:].bitcast(I32), source[0].bitcast(I32))
+            ww_raw.append(part)
+        for w, source in enumerate((w3_scales, w4_scales, w2_scales)):
+            nc.sync.dma_start(ws_raw[0:16, w, :].bitcast(I32), source[0].bitcast(I32))
+        gate_near = keep.tile([P, D, V], F32, name="gate_near")
+        nc.sync.dma_start(gate_near[:], gate.rearrange("d p v -> p d v"))
+        near += [load_list("pos1_t", pos2), load_list("pos2_t", pos3)]
+        far = [load_list("far%d_t" % d, source) for d, source in enumerate((far1, far2, far3))]
+        gate_far = keep.tile([P, D, V], F32, name="gate_far")
+        nc.sync.dma_start(gate_far[:], gate2.rearrange("d p v -> p d v"))
+        cen_t = load_list("cen_t", cen)
+
+        xq_words = keep.tile([P, S], U32, name="xq_words", align_bytes=64)
+        nc.vector.tensor_copy(xq_words[:], xw[:].indirect(offs_t[:]))
+        xq_scales = keep.tile([P, S], U8, name="xq_scales", align_bytes=64)
+        nc.vector.tensor_copy(xq_scales[:], xs[:].indirect(offs_t[:]))
+
+        w1_bf = keep.tile([P, PACK, P, PACK], BF16, name="w1_bf", align_bytes=64)
+
+        def deal_w1(q, m0, m1, on_scalar):
+            dst = w1_bf[:, :, 32 * q + m0 : 32 * q + m1, :].rearrange("p t m j -> p m j t")
+            src = w1_raw[q][:, :, PACK * m0 : PACK * m1].rearrange("p j (m t) -> p m j t", t=PACK)
+            if on_scalar:
+                nc.scalar.activation(out=dst, in_=src, func=ACT.Copy)
+            else:
+                nc.vector.tensor_copy(dst, src)
+
+        for q in range(3):
+            deal_w1(q, 0, 32, True)
+        deal_w1(3, 0, 32, True)
+        h = []
+        h_banks = []
+        for t in range(PACK):
+            codes = keep.tile([P, P], U32, name="w1_codes%d" % t, align_bytes=64)
+            scales = keep.tile([P, P], U8, name="w1_scales%d" % t, align_bytes=64)
+            nc.vector.quantize_mx(out=codes[:].bitcast(FP8X4), scales=scales[:], in_=w1_bf[:, t].rearrange("p m j -> p (m j)"))
+            bank = acc.tile([P, S], F32, name="bank%d" % t)
+            nc.tensor.matmul_mx(out=bank[:], lhsT=codes[:].bitcast(FP8X4), lhsT_scale=scales[:],
+                                rhs=xq_words[:].bitcast(FP8X4), rhs_scale=xq_scales[:], start=True, stop=True)
+            h_banks.append(bank)
+            h.append(keep.tile([P, S], F32, name="h%d" % t))
+        for t in range(PACK):
+            nc.scalar.activation(out=h[t][:], in_=h_banks[t][:], func=ACT.Relu)
+
+        ww = []
+        for w in range(3):
+            dealt = keep.tile([P, 2 * N], U8, name="ww%d" % w, align_bytes=64)
+            nc.scalar.copy(dealt[:].bitcast(U16).rearrange("p (t m) -> p t m", t=PACK),
+                           ww_raw[w][:].bitcast(U16).rearrange("p (m t) -> p t m", t=PACK))
+            ww.append(dealt)
+        ws = keep.tile([P, 3, N], U8, name="ws", align_bytes=64)
+        nc.vector.tensor_copy(ws[:].rearrange("p w (t m) -> p w t m", t=PACK), ws_raw[:].rearrange("p w (m t) -> p w t m", t=PACK))
+        ws_rows = ws[:].rearrange("p w n -> p (w n)").bitcast(I32)
+        for q in range(1, 4):
+            nc.sync.dma_start(ws_rows[32 * q : 32 * q + 4, :], ws_rows[4 * q : 4 * q + 4, :])
+
+        y_words = keep.tile([P, V], U32, name="y_words", align_bytes=64)
+        y_scales = keep.tile([P, V], U8, name="y_scales", align_bytes=64)
+        out_rows = out_0.rearrange("(p t) v -> p t v", t=PACK)
+        out_words = out_1[0].rearrange("p v t -> p (v t)").bitcast(I32)
+
+        def offsets(tile, half):
+            return tile[:, half * COLS : (half + 1) * COLS]
+
+        def fetch_plain(lists, half, counts):
+            plain = ring.tile([P, D, PACK, HALF], F32, name="plain", bufs=2)
+            for t in range(PACK):
+                for d in range(D):
+                    if t >= PACK - counts[d]:
+                        nc.scalar.activation(out=plain[:, d, t, :], in_=h[t][:].indirect(offsets(lists[d], half)), func=ACT.Copy)
+            return plain
+
+        def weigh(plain, lists, gates, half, counts, at):
+            cols = slice(half * HALF, (half + 1) * HALF)
+            terms = ring.tile([P, D, PACK, HALF], F32, name="terms")
+            for t in range(PACK + 1):
+                if t == at:
+                    for d in range(D):
+                        if counts[d]:
+                            nc.vector.tensor_tensor(terms[:, d, PACK - counts[d] :, :], plain[:, d, PACK - counts[d] :, :],
+                                                    gates[:, d : d + 1, cols].to_broadcast([P, counts[d], HALF]), ALU.mult)
+                for d in range(D):
+                    if t < PACK - counts[d]:
+                        nc.vector.tensor_tensor(terms[:, d, t, :], h[t][:].indirect(offsets(lists[d], half)), gates[:, d, cols], ALU.mult)
+            return [terms[:, d] for d in range(D)]
+
+        def add_turned(terms):
+            total = turn.tile([P, PACK, P], F32, name="total")
+            for t in range(PACK):
+                for d in reversed(range(D)):
+                    nc.tensor.matmul(total[:, t, :], lhsT=terms[d][:, t, :], rhs=ident[:], is_transpose=True, start=(d == D - 1), stop=(d == 0))
+            return total
+
+        def weigh_and_add(plain, lists, gates, half, counts, between):
+            cols = slice(half * HALF, (half + 1) * HALF)
+            terms = ring.tile([P, D, PACK, HALF], F32, name="terms")
+            two = ring.tile([P, PACK, HALF], F32, name="two")
+            for d in reversed(range(D)):
+                if counts[d]:
+                    nc.vector.tensor_tensor(terms[:, d, PACK - counts[d] :, :], plain[:, d, PACK - counts[d] :, :],
+                                            gates[:, d : d + 1, cols].to_broadcast([P, counts[d], HALF]), ALU.mult)
+            for d in reversed(range(D)):
+                for t in range(PACK - counts[d]):
+                    nc.vector.tensor_tensor(terms[:, d, t, :], h[t][:].indirect(offsets(lists[d], half)), gates[:, d, cols], ALU.mult)
+                    if d == 0 and t == 0:
+                        nc.vector.tensor_tensor(two[:], terms[:, 1], terms[:, 2], ALU.add)
+            between()
+            z = ring.tile([P, HALF * PACK], BF16, name="z", align_bytes=64, bufs=6)
+            nc.vector.tensor_tensor(z[:].rearrange("p (c i t) -> p c t i", i=4, t=PACK), terms[:, 0].rearrange("p t (c i) -> p c t i", i=4),
+                                    two[:].rearrange("p t (c i) -> p c t i", i=4), ALU.add)
+            return z
+
+        def turn_back(total):
+            pairs = ring.tile([P, 2, P, 2], BF16, name="pairs")
+            nc.scalar.activation(out=pairs[:], in_=total[:].rearrange("v (u e) p -> v u p e", e=2), func=ACT.Copy)
+            words = pairs[:].rearrange("v u p e -> v u (p e)").bitcast(F32)
+            back = turn.tile([P, 2, HALF], F32, name="back")
+            for u in range(2):
+                nc.tensor.transpose(back[:, u, :], words[:, u, :], ident[:])
+            return back
+
+        def weave_back(back):
+            z = ring.tile([P, HALF * PACK], BF16, name="z", align_bytes=64, bufs=6)
+            nc.scalar.copy(z[:].bitcast(F32).rearrange("p (v u) -> p v u", u=2), back[:].rearrange("p u v -> p v u"))
+            return z
+
+        def gather_own(half, on_scalar):
+            own = ring.tile([P, PACK, HALF], BF16, name="own")
+            for t in range(PACK):
+                if t < on_scalar:
+                    nc.scalar.activation(out=own[:, t, :], in_=h[t][:].indirect(offsets(cen_t, half)), func=ACT.Copy)
+                else:
+                    nc.vector.tensor_copy(own[:, t, :], h[t][:].indirect(offsets(cen_t, half)))
+            return own
+
+        def weave_own(own):
+            z = ring.tile([P, HALF * PACK], BF16, name="z", align_bytes=64, bufs=6)
+            nc.vector.tensor_copy(z[:].rearrange("p (c i t) -> p c t i", i=4, t=PACK), own[:].rearrange("p t (c i) -> p c t i", i=4))
+            return z
+
+        def multiply(z, w, banks, first, last):
+            codes = ring.tile([P, HALF], U32, name="z_codes", align_bytes=64, bufs=6)
+            scales = ring.tile([P, HALF], U8, name="z_scales", align_bytes=64, bufs=6)
+            nc.vector.quantize_mx(out=codes[:].bitcast(FP8X4), scales=scales[:], in_=z[:])
+            for t in range(PACK):
+                nc.tensor.matmul_mx(out=banks[t // 2][:, t % 2, :], lhsT=ww[w][:, 2 * P * t : 2 * P * (t + 1)].bitcast(FP4X4),
+                                    lhsT_scale=ws[:, w, P * t : P * (t + 1)], rhs=codes[:].bitcast(FP8X4), rhs_scale=scales[:],
+                                    start=(first and t % 2 == 0), stop=(last and t % 2 == 1))
+
+        def hand_out(banks, half, both):
+            cols = slice(half * HALF, (half + 1) * HALF)
+            y = ring.tile([P, PACK, HALF], F32, name="y")
+            nc.scalar.copy(y[:, 0:2, :], banks[0][:])
+            if both:
+                nc.vector.tensor_copy(y[:, 2:4, :], banks[1][:])
+            else:
+                nc.scalar.copy(y[:, 2:4, :], banks[1][:])
+            nc.sync.dma_start(out_rows[:, :, cols], y[:])
+            y_bf = ring.tile([P, HALF * PACK], BF16, name="y_bf", align_bytes=64)
+            nc.vector.tensor_copy(y_bf[:].rearrange("p (c i t) -> p c t i", i=4, t=PACK), y[:].rearrange("p t (c i) -> p c t i", i=4))
+            nc.vector.quantize_mx(out=y_words[:, cols].bitcast(FP8X4), scales=y_scales[:, cols], in_=y_bf[:])
+            nc.sync.dma_start(out_words[:, cols], y_words[:, cols].bitcast(I32))
+
+        def out_banks(half):
+            return [acc.tile([P, 2, HALF], F32, name="bank%d" % (2 * half + u)) for u in range(2)]
+
+        plain_a1 = None
+        plain_b1 = fetch_plain(near, 1, (0, 1, 4))
+        total_a1 = add_turned(weigh(plain_a1, near, gate_near, 0, (0, 0, 0), 4))
+        plain_a2 = fetch_plain(far, 0, (0, 3, 4))
+        back_a1 = turn_back(total_a1)
+        total_b1 = add_turned(weigh(plain_b1, near, gate_near, 1, (0, 1, 4), 0))
+        banks_a = out_banks(0)
+        banks_b = out_banks(1)
+        z_a1 = weave_back(back_a1)
+        plain_b2 = fetch_plain(far, 1, (0, 4, 4))
+        back_b1 = turn_back(total_b1)
+        total_a2 = add_turned(weigh(plain_a2, far, gate_far, 0, (0, 3, 4), 0))
+        multiply(z_a1, 0, banks_a, True, False)
+        z_b1 = weave_back(back_b1)
+        own_a = gather_own(0, 4)
+        back_a2 = turn_back(total_a2)
+        own_b = gather_own(1, 4)
+        z_a2 = weave_back(back_a2)
+        multiply(z_b1, 0, banks_b, True, False)
+        z_a0 = weave_own(own_a)
+        z_b2 = weigh_and_add(plain_b2, far, gate_far, 1, (0, 4, 4), lambda: [multiply(z_a0, 2, banks_a, False, False), multiply(z_a2, 1, banks_a, False, True)])
+        z_b0 = weave_own(own_b)
+        multiply(z_b2, 1, banks_b, False, False)
+        multiply(z_b0, 2, banks_b, False, True)
+        hand_out(banks_a, 0, False)
+        hand_out(banks_b, 1, True)
+        for q in range(4):
+            queue = nc.sync if q % 2 == 0 else nc.scalar
+            queue.dma_start(out_2[0, 4 * q : 4 * q + 4, :].bitcast(I32), y_scales[32 * q : 32 * q + 4, :].bitcast(I32))

@@ -20,7 +20,9 @@ ALU = mybir.AluOpType
 P = 128
 PACK = 4
 HALF = 128
-COLS = HALF // 16
+HALVES = (slice(0, HALF), slice(HALF, V))
+WHOLE = slice(0, V)
+W1_PARTS = ((0, 48), (48, 96), (96, 128))
 
 
 def tile_picked_zmix_none_po_kernel(
@@ -30,7 +32,7 @@ def tile_picked_zmix_none_po_kernel(
     nc = tc.nc
     with ExitStack() as ctx:
         keep = ctx.enter_context(tc.tile_pool(name="keep", bufs=1))
-        ring = ctx.enter_context(tc.tile_pool(name="ring", bufs=4))
+        ring = ctx.enter_context(tc.tile_pool(name="ring", bufs=2))
         acc = ctx.enter_context(tc.psum_pool(name="acc", bufs=1))
         turn = ctx.enter_context(tc.psum_pool(name="turn", bufs=2))
 
@@ -40,37 +42,42 @@ def tile_picked_zmix_none_po_kernel(
             return tile
 
         xs = keep.tile([P, T], U8, name="xs", align_bytes=64)
-        nc.vector.memset(xs[:].bitcast(I32), 0)
-        ws_raw = keep.tile([P, 3, N], U8, name="ws_raw", align_bytes=64)
-        nc.gpsimd.memset(ws_raw[:].rearrange("p w n -> p (w n)").bitcast(I32), 0)
+        nc.gpsimd.memset(xs[:].bitcast(I32), 0)
+        ws_raw = keep.tile([P, N], U8, name="ws_raw", align_bytes=64)
+        nc.gpsimd.memset(ws_raw[:].bitcast(I32), 0)
+        ws = keep.tile([P, 3, N], U8, name="ws", align_bytes=64)
+        nc.gpsimd.memset(ws[:].rearrange("p w n -> p (w n)").bitcast(I32), 0)
         ident = keep.tile([P, P], F32, name="ident")
         make_identity(nc, ident[:])
 
+        def load_gate(name, source):
+            tile = keep.tile([P, D, V], F32, name=name)
+            nc.sync.dma_start(tile[:], source.rearrange("d p v -> p d v"))
+            return tile
+
+        def load_words(name, source):
+            tile = keep.tile([P, 2 * N], U8, name=name, align_bytes=64)
+            nc.sync.dma_start(tile[:].bitcast(I32), source[0].bitcast(I32))
+            return tile
+
         offs_t = load_list("offs_t", offs)
-        near = [load_list("pos0_t", pos1)]
         for q in range(4):
             nc.scalar.dma_start(xs[32 * q : 32 * q + 4, :].bitcast(I32), x_scales[0, 4 * q : 4 * q + 4, :].bitcast(I32))
         xw = keep.tile([P, T], U32, name="xw", align_bytes=64)
         nc.sync.dma_start(xw[:].bitcast(I32), x_words[0].rearrange("p n t -> p (n t)").bitcast(I32))
         w1_rows = w1.rearrange("(p j) c -> p j c", j=PACK)
         w1_raw = []
-        for q in range(4):
-            part = keep.tile([P, PACK, P], F32, name="w1_raw%d" % q)
-            nc.sync.dma_start(part[:], w1_rows[:, :, q * P : (q + 1) * P])
+        for q, (m0, m1) in enumerate(W1_PARTS):
+            part = keep.tile([P, PACK, PACK * (m1 - m0)], F32, name="w1_raw%d" % q, align_bytes=64)
+            nc.sync.dma_start(part[:], w1_rows[:, :, PACK * m0 : PACK * m1])
             w1_raw.append(part)
-        ww_raw = []
-        for w, source in enumerate((w3_words, w4_words, w2_words)):
-            part = keep.tile([P, 2 * N], U8, name="ww_raw%d" % w, align_bytes=64)
-            nc.sync.dma_start(part[:].bitcast(I32), source[0].bitcast(I32))
-            ww_raw.append(part)
+        near = [load_list("pos%d_t" % d, source) for d, source in enumerate((pos1, pos2, pos3))]
+        gate_near = load_gate("gate_near", gate)
+        ww_raw = [load_words("w%d_raw" % w, source) for w, source in enumerate((w3_words, w4_words, w2_words))]
         for w, source in enumerate((w3_scales, w4_scales, w2_scales)):
-            nc.sync.dma_start(ws_raw[0:16, w, :].bitcast(I32), source[0].bitcast(I32))
-        gate_near = keep.tile([P, D, V], F32, name="gate_near")
-        nc.sync.dma_start(gate_near[:], gate.rearrange("d p v -> p d v"))
-        near += [load_list("pos1_t", pos2), load_list("pos2_t", pos3)]
+            nc.sync.dma_start(ws_raw[16 * w : 16 * (w + 1), :].bitcast(I32), source[0].bitcast(I32))
         far = [load_list("far%d_t" % d, source) for d, source in enumerate((far1, far2, far3))]
-        gate_far = keep.tile([P, D, V], F32, name="gate_far")
-        nc.sync.dma_start(gate_far[:], gate2.rearrange("d p v -> p d v"))
+        gate_far = load_gate("gate_far", gate2)
         cen_t = load_list("cen_t", cen)
 
         xq_words = keep.tile([P, S], U32, name="xq_words", align_bytes=64)
@@ -78,19 +85,20 @@ def tile_picked_zmix_none_po_kernel(
         xq_scales = keep.tile([P, S], U8, name="xq_scales", align_bytes=64)
         nc.vector.tensor_copy(xq_scales[:], xs[:].indirect(offs_t[:]))
 
-        w1_bf = keep.tile([P, PACK, P, PACK], BF16, name="w1_bf", align_bytes=64)
+        w1_bf = keep.tile([P, PACK, P, PACK], BF16, name="w1_bf", tag="dealt", align_bytes=64)
 
         def deal_w1(q, m0, m1, on_scalar):
-            dst = w1_bf[:, :, 32 * q + m0 : 32 * q + m1, :].rearrange("p t m j -> p m j t")
-            src = w1_raw[q][:, :, PACK * m0 : PACK * m1].rearrange("p j (m t) -> p m j t", t=PACK)
+            first = W1_PARTS[q][0]
+            dst = w1_bf[:, :, m0:m1, :].rearrange("p t m j -> p m j t")
+            src = w1_raw[q][:, :, PACK * (m0 - first) : PACK * (m1 - first)].rearrange("p j (m t) -> p m j t", t=PACK)
             if on_scalar:
                 nc.scalar.activation(out=dst, in_=src, func=ACT.Copy)
             else:
                 nc.vector.tensor_copy(dst, src)
 
-        for q in range(3):
-            deal_w1(q, 0, 32, True)
-        deal_w1(3, 0, 32, True)
+        deal_w1(0, 0, 48, True)
+        deal_w1(1, 48, 96, True)
+        deal_w1(2, 96, 128, True)
         h = []
         h_banks = []
         for t in range(PACK):
@@ -105,79 +113,77 @@ def tile_picked_zmix_none_po_kernel(
         for t in range(PACK):
             nc.scalar.activation(out=h[t][:], in_=h_banks[t][:], func=ACT.Relu)
 
-        ww = []
+        ww = keep.tile([P, 3, 2 * N], U8, name="ww", tag="w1_raw2", align_bytes=64)
         for w in range(3):
-            dealt = keep.tile([P, 2 * N], U8, name="ww%d" % w, align_bytes=64)
-            nc.scalar.copy(dealt[:].bitcast(U16).rearrange("p (t m) -> p t m", t=PACK),
+            nc.scalar.copy(ww[:, w, :].bitcast(U16).rearrange("p (t m) -> p t m", t=PACK),
                            ww_raw[w][:].bitcast(U16).rearrange("p (m t) -> p t m", t=PACK))
-            ww.append(dealt)
-        ws = keep.tile([P, 3, N], U8, name="ws", align_bytes=64)
-        nc.vector.tensor_copy(ws[:].rearrange("p w (t m) -> p w t m", t=PACK), ws_raw[:].rearrange("p w (m t) -> p w t m", t=PACK))
-        ws_rows = ws[:].rearrange("p w n -> p (w n)").bitcast(I32)
-        for q in range(1, 4):
-            nc.sync.dma_start(ws_rows[32 * q : 32 * q + 4, :], ws_rows[4 * q : 4 * q + 4, :])
+        ws_dealt = keep.tile([P, N], U8, name="ws_dealt", tag="dealt", align_bytes=64)
+        nc.vector.tensor_copy(ws_dealt[:].rearrange("p (t m) -> p t m", t=PACK), ws_raw[:].rearrange("p (m t) -> p t m", t=PACK))
+        for w in range(3):
+            for q in range(4):
+                row = 16 * w + 4 * q
+                nc.sync.dma_start(ws[32 * q : 32 * q + 4, w, :].bitcast(I32), ws_dealt[row : row + 4, :].bitcast(I32))
 
         y_words = keep.tile([P, V], U32, name="y_words", align_bytes=64)
         y_scales = keep.tile([P, V], U8, name="y_scales", align_bytes=64)
         out_rows = out_0.rearrange("(p t) v -> p t v", t=PACK)
         out_words = out_1[0].rearrange("p v t -> p (v t)").bitcast(I32)
 
-        def offsets(tile, half):
-            return tile[:, half * COLS : (half + 1) * COLS]
+        own = keep.tile([P, PACK, V], BF16, name="own")
 
-        def fetch_plain(lists, half, counts):
-            plain = ring.tile([P, D, PACK, HALF], F32, name="plain", bufs=2)
+        def offsets(tile, cols):
+            return tile[:, cols.start // 16 : cols.stop // 16]
+
+        def fetch_plain(lists, counts):
+            plain = ring.tile([P, PACK, D, V], F32, name="plain")
             for t in range(PACK):
-                for d in range(D):
-                    if t >= PACK - counts[d]:
-                        nc.scalar.activation(out=plain[:, d, t, :], in_=h[t][:].indirect(offsets(lists[d], half)), func=ACT.Copy)
+                for d in range(D - counts[t], D):
+                    nc.scalar.activation(out=plain[:, t, d, :], in_=h[t][:].indirect(lists[d][:]), func=ACT.Copy)
             return plain
 
-        def weigh(plain, lists, gates, half, counts, at):
-            cols = slice(half * HALF, (half + 1) * HALF)
-            terms = ring.tile([P, D, PACK, HALF], F32, name="terms")
-            for t in range(PACK + 1):
-                if t == at:
-                    for d in range(D):
-                        if counts[d]:
-                            nc.vector.tensor_tensor(terms[:, d, PACK - counts[d] :, :], plain[:, d, PACK - counts[d] :, :],
-                                                    gates[:, d : d + 1, cols].to_broadcast([P, counts[d], HALF]), ALU.mult)
-                for d in range(D):
-                    if t < PACK - counts[d]:
-                        nc.vector.tensor_tensor(terms[:, d, t, :], h[t][:].indirect(offsets(lists[d], half)), gates[:, d, cols], ALU.mult)
-            return [terms[:, d] for d in range(D)]
+        def weigh_plain(terms, plain, gates, cols, t, count):
+            if count:
+                nc.vector.tensor_tensor(terms[:, t, D - count :, cols], plain[:, t, D - count :, cols], gates[:, D - count :, cols], ALU.mult)
 
-        def add_turned(terms):
-            total = turn.tile([P, PACK, P], F32, name="total")
+        def fetch_weighed(terms, lists, gates, cols, t, d):
+            nc.vector.tensor_tensor(terms[:, t, d, cols], h[t][:].indirect(offsets(lists[d], cols)), gates[:, d, cols], ALU.mult)
+
+        def weigh(terms, plain, lists, gates, cols, counts):
             for t in range(PACK):
-                for d in reversed(range(D)):
-                    nc.tensor.matmul(total[:, t, :], lhsT=terms[d][:, t, :], rhs=ident[:], is_transpose=True, start=(d == D - 1), stop=(d == 0))
-            return total
+                for d in range(D - counts[t]):
+                    fetch_weighed(terms, lists, gates, cols, t, d)
+                weigh_plain(terms, plain, gates, cols, t, counts[t])
 
-        def weigh_and_add(plain, lists, gates, half, counts, between):
-            cols = slice(half * HALF, (half + 1) * HALF)
-            terms = ring.tile([P, D, PACK, HALF], F32, name="terms")
+        def add_turned(terms, halves):
+            totals = [turn.tile([P, PACK, P], F32, name="total", bufs=2) for half in halves]
+            for t in range(PACK):
+                for total, half in zip(totals, halves):
+                    for d in range(D):
+                        nc.tensor.matmul(total[:, t, :], lhsT=terms[:, t, d, HALVES[half]], rhs=ident[:], is_transpose=True,
+                                         start=(d == 0), stop=(d == D - 1))
+            return totals
+
+        def weigh_and_add(terms, plain, lists, gates, cols, counts, between):
             two = ring.tile([P, PACK, HALF], F32, name="two")
+            for t in range(PACK):
+                weigh_plain(terms, plain, gates, cols, t, counts[t])
             for d in reversed(range(D)):
-                if counts[d]:
-                    nc.vector.tensor_tensor(terms[:, d, PACK - counts[d] :, :], plain[:, d, PACK - counts[d] :, :],
-                                            gates[:, d : d + 1, cols].to_broadcast([P, counts[d], HALF]), ALU.mult)
-            for d in reversed(range(D)):
-                for t in range(PACK - counts[d]):
-                    nc.vector.tensor_tensor(terms[:, d, t, :], h[t][:].indirect(offsets(lists[d], half)), gates[:, d, cols], ALU.mult)
+                for t in range(PACK):
+                    if d < D - counts[t]:
+                        fetch_weighed(terms, lists, gates, cols, t, d)
                     if d == 0 and t == 0:
-                        nc.vector.tensor_tensor(two[:], terms[:, 1], terms[:, 2], ALU.add)
+                        nc.vector.tensor_tensor(two[:], terms[:, :, 1, cols], terms[:, :, 2, cols], ALU.add)
             between()
             z = ring.tile([P, HALF * PACK], BF16, name="z", align_bytes=64, bufs=6)
-            nc.vector.tensor_tensor(z[:].rearrange("p (c i t) -> p c t i", i=4, t=PACK), terms[:, 0].rearrange("p t (c i) -> p c t i", i=4),
+            nc.vector.tensor_tensor(z[:].rearrange("p (c i t) -> p c t i", i=4, t=PACK), terms[:, :, 0, cols].rearrange("p t (c i) -> p c t i", i=4),
                                     two[:].rearrange("p t (c i) -> p c t i", i=4), ALU.add)
             return z
 
         def turn_back(total):
-            pairs = ring.tile([P, 2, P, 2], BF16, name="pairs")
+            pairs = ring.tile([P, 2, P, 2], BF16, name="pairs", bufs=3)
             nc.scalar.activation(out=pairs[:], in_=total[:].rearrange("v (u e) p -> v u p e", e=2), func=ACT.Copy)
             words = pairs[:].rearrange("v u p e -> v u (p e)").bitcast(F32)
-            back = turn.tile([P, 2, HALF], F32, name="back")
+            back = turn.tile([P, 2, HALF], F32, name="back", bufs=2)
             for u in range(2):
                 nc.tensor.transpose(back[:, u, :], words[:, u, :], ident[:])
             return back
@@ -187,26 +193,24 @@ def tile_picked_zmix_none_po_kernel(
             nc.scalar.copy(z[:].bitcast(F32).rearrange("p (v u) -> p v u", u=2), back[:].rearrange("p u v -> p v u"))
             return z
 
-        def gather_own(half, on_scalar):
-            own = ring.tile([P, PACK, HALF], BF16, name="own")
+        def gather_own(cols, on_scalar):
             for t in range(PACK):
                 if t < on_scalar:
-                    nc.scalar.activation(out=own[:, t, :], in_=h[t][:].indirect(offsets(cen_t, half)), func=ACT.Copy)
+                    nc.scalar.activation(out=own[:, t, cols], in_=h[t][:].indirect(offsets(cen_t, cols)), func=ACT.Copy)
                 else:
-                    nc.vector.tensor_copy(own[:, t, :], h[t][:].indirect(offsets(cen_t, half)))
-            return own
+                    nc.vector.tensor_copy(own[:, t, cols], h[t][:].indirect(offsets(cen_t, cols)))
 
-        def weave_own(own):
-            z = ring.tile([P, HALF * PACK], BF16, name="z", align_bytes=64, bufs=6)
-            nc.vector.tensor_copy(z[:].rearrange("p (c i t) -> p c t i", i=4, t=PACK), own[:].rearrange("p t (c i) -> p c t i", i=4))
-            return z
+        def weave(copy, source, name):
+            woven = ring.tile([P, HALF * PACK], BF16, name=name, align_bytes=64, bufs=6)
+            copy(woven[:].rearrange("p (c i t) -> p c t i", i=4, t=PACK), source.rearrange("p t (c i) -> p c t i", i=4))
+            return woven
 
         def multiply(z, w, banks, first, last):
             codes = ring.tile([P, HALF], U32, name="z_codes", align_bytes=64, bufs=6)
             scales = ring.tile([P, HALF], U8, name="z_scales", align_bytes=64, bufs=6)
             nc.vector.quantize_mx(out=codes[:].bitcast(FP8X4), scales=scales[:], in_=z[:])
             for t in range(PACK):
-                nc.tensor.matmul_mx(out=banks[t // 2][:, t % 2, :], lhsT=ww[w][:, 2 * P * t : 2 * P * (t + 1)].bitcast(FP4X4),
+                nc.tensor.matmul_mx(out=banks[t // 2][:, t % 2, :], lhsT=ww[:, w, 2 * P * t : 2 * P * (t + 1)].bitcast(FP4X4),
                                     lhsT_scale=ws[:, w, P * t : P * (t + 1)], rhs=codes[:].bitcast(FP8X4), rhs_scale=scales[:],
                                     start=(first and t % 2 == 0), stop=(last and t % 2 == 1))
 
@@ -219,38 +223,37 @@ def tile_picked_zmix_none_po_kernel(
             else:
                 nc.scalar.copy(y[:, 2:4, :], banks[1][:])
             nc.sync.dma_start(out_rows[:, :, cols], y[:])
-            y_bf = ring.tile([P, HALF * PACK], BF16, name="y_bf", align_bytes=64)
-            nc.vector.tensor_copy(y_bf[:].rearrange("p (c i t) -> p c t i", i=4, t=PACK), y[:].rearrange("p t (c i) -> p c t i", i=4))
+            y_bf = weave(nc.vector.tensor_copy if both or not False else nc.scalar.copy, y[:], "y_bf")
             nc.vector.quantize_mx(out=y_words[:, cols].bitcast(FP8X4), scales=y_scales[:, cols], in_=y_bf[:])
             nc.sync.dma_start(out_words[:, cols], y_words[:, cols].bitcast(I32))
 
         def out_banks(half):
             return [acc.tile([P, 2, HALF], F32, name="bank%d" % (2 * half + u)) for u in range(2)]
 
-        plain_a1 = None
-        plain_b1 = fetch_plain(near, 1, (0, 1, 4))
-        total_a1 = add_turned(weigh(plain_a1, near, gate_near, 0, (0, 0, 0), 4))
-        plain_a2 = fetch_plain(far, 0, (0, 3, 4))
+        plain_near = fetch_plain(near, (0, 0, 1, 1))
+        terms_near = ring.tile([P, PACK, D, V], F32, name="terms")
+        weigh(terms_near, plain_near, near, gate_near, WHOLE, (0, 0, 1, 1))
+        total_a1, total_b1 = add_turned(terms_near, (0, 1))
+        plain_far = fetch_plain(far, (2, 2, 2, 1))
+        terms_far = ring.tile([P, PACK, D, V], F32, name="terms")
         back_a1 = turn_back(total_a1)
-        total_b1 = add_turned(weigh(plain_b1, near, gate_near, 1, (0, 1, 4), 0))
+        back_b1 = turn_back(total_b1)
         banks_a = out_banks(0)
         banks_b = out_banks(1)
         z_a1 = weave_back(back_a1)
-        plain_b2 = fetch_plain(far, 1, (0, 4, 4))
-        back_b1 = turn_back(total_b1)
-        total_a2 = add_turned(weigh(plain_a2, far, gate_far, 0, (0, 3, 4), 0))
-        multiply(z_a1, 0, banks_a, True, False)
+        weigh(terms_far, plain_far, far, gate_far, HALVES[0], (2, 2, 2, 1))
+        total_a2, = add_turned(terms_far, (0,))
+        gather_own(HALVES[0], 4)
         z_b1 = weave_back(back_b1)
-        own_a = gather_own(0, 4)
+        multiply(z_a1, 0, banks_a, True, False)
         back_a2 = turn_back(total_a2)
-        own_b = gather_own(1, 4)
+        z_a0 = weave(nc.scalar.copy, own[:, :, HALVES[0]], "z")
         z_a2 = weave_back(back_a2)
+        gather_own(HALVES[1], 2)
         multiply(z_b1, 0, banks_b, True, False)
-        z_a0 = weave_own(own_a)
-        z_b2 = weigh_and_add(plain_b2, far, gate_far, 1, (0, 4, 4), lambda: [multiply(z_a0, 2, banks_a, False, False), multiply(z_a2, 1, banks_a, False, True)])
-        z_b0 = weave_own(own_b)
-        multiply(z_b2, 1, banks_b, False, False)
-        multiply(z_b0, 2, banks_b, False, True)
+        z_b2 = weigh_and_add(terms_far, plain_far, far, gate_far, HALVES[1], (2, 2, 2, 1), lambda: [multiply(z_a0, 2, banks_a, False, False), multiply(z_a2, 1, banks_a, False, True)])
+        multiply(weave(nc.vector.tensor_copy, own[:, :, HALVES[1]], "z"), 2, banks_b, False, False)
+        multiply(z_b2, 1, banks_b, False, True)
         hand_out(banks_a, 0, False)
         hand_out(banks_b, 1, True)
         for q in range(4):

@@ -22,7 +22,7 @@ PACK = 4
 HALF = 128
 HALVES = (slice(0, HALF), slice(HALF, V))
 WHOLE = slice(0, V)
-W1_PARTS = ((0, 48), (48, 96), (96, 128))
+W1_PARTS = ((0, 64), (64, 128))
 
 
 def tile_picked_zmix_none_po_kernel(
@@ -45,6 +45,8 @@ def tile_picked_zmix_none_po_kernel(
         nc.gpsimd.memset(xs[:].bitcast(I32), 0)
         ws_raw = keep.tile([P, N], U8, name="ws_raw", align_bytes=64)
         nc.gpsimd.memset(ws_raw[:].bitcast(I32), 0)
+        for w, source in enumerate((w3_scales, w4_scales, w2_scales)):
+            nc.gpsimd.dma_start(ws_raw[16 * w : 16 * (w + 1), :].bitcast(I32), source[0].bitcast(I32))
         ws = keep.tile([P, 3, N], U8, name="ws", align_bytes=64)
         nc.gpsimd.memset(ws[:].rearrange("p w n -> p (w n)").bitcast(I32), 0)
         ident = keep.tile([P, P], F32, name="ident")
@@ -62,7 +64,7 @@ def tile_picked_zmix_none_po_kernel(
 
         offs_t = load_list("offs_t", offs)
         for q in range(4):
-            nc.scalar.dma_start(xs[32 * q : 32 * q + 4, :].bitcast(I32), x_scales[0, 4 * q : 4 * q + 4, :].bitcast(I32))
+            (nc.sync if q < 2 else nc.scalar).dma_start(xs[32 * q : 32 * q + 4, :].bitcast(I32), x_scales[0, 4 * q : 4 * q + 4, :].bitcast(I32))
         xw = keep.tile([P, T], U32, name="xw", align_bytes=64)
         nc.sync.dma_start(xw[:].bitcast(I32), x_words[0].rearrange("p n t -> p (n t)").bitcast(I32))
         w1_rows = w1.rearrange("(p j) c -> p j c", j=PACK)
@@ -72,10 +74,8 @@ def tile_picked_zmix_none_po_kernel(
             nc.sync.dma_start(part[:], w1_rows[:, :, PACK * m0 : PACK * m1])
             w1_raw.append(part)
         near = [load_list("pos%d_t" % d, source) for d, source in enumerate((pos1, pos2, pos3))]
-        gate_near = load_gate("gate_near", gate)
         ww_raw = [load_words("w%d_raw" % w, source) for w, source in enumerate((w3_words, w4_words, w2_words))]
-        for w, source in enumerate((w3_scales, w4_scales, w2_scales)):
-            nc.sync.dma_start(ws_raw[16 * w : 16 * (w + 1), :].bitcast(I32), source[0].bitcast(I32))
+        gate_near = load_gate("gate_near", gate)
         far = [load_list("far%d_t" % d, source) for d, source in enumerate((far1, far2, far3))]
         gate_far = load_gate("gate_far", gate2)
         cen_t = load_list("cen_t", cen)
@@ -96,24 +96,28 @@ def tile_picked_zmix_none_po_kernel(
             else:
                 nc.vector.tensor_copy(dst, src)
 
-        deal_w1(0, 0, 48, True)
-        deal_w1(1, 48, 96, True)
-        deal_w1(2, 96, 128, True)
+        deal_w1(0, 0, 64, True)
+        deal_w1(1, 64, 86, True)
+        deal_w1(1, 86, 128, False)
         h = []
         h_banks = []
         for t in range(PACK):
             codes = keep.tile([P, P], U32, name="w1_codes%d" % t, align_bytes=64)
             scales = keep.tile([P, P], U8, name="w1_scales%d" % t, align_bytes=64)
             nc.vector.quantize_mx(out=codes[:].bitcast(FP8X4), scales=scales[:], in_=w1_bf[:, t].rearrange("p m j -> p (m j)"))
-            bank = acc.tile([P, S], F32, name="bank%d" % t)
-            nc.tensor.matmul_mx(out=bank[:], lhsT=codes[:].bitcast(FP8X4), lhsT_scale=scales[:],
-                                rhs=xq_words[:].bitcast(FP8X4), rhs_scale=xq_scales[:], start=True, stop=True)
-            h_banks.append(bank)
             h.append(keep.tile([P, S], F32, name="h%d" % t))
-        for t in range(PACK):
-            nc.scalar.activation(out=h[t][:], in_=h_banks[t][:], func=ACT.Relu)
+            if t == 0:
+                parts = [(turn.tile([P, S // 2], F32, name="back", bufs=2), slice(0, S // 2)), (acc.tile([P, S // 2], F32, name="bank0"), slice(S // 2, S))]
+            else:
+                parts = [(acc.tile([P, S], F32, name="bank%d" % t), slice(0, S))]
+            for bank, cols in parts:
+                nc.tensor.matmul_mx(out=bank[:], lhsT=codes[:].bitcast(FP8X4), lhsT_scale=scales[:],
+                                    rhs=xq_words[:, cols].bitcast(FP8X4), rhs_scale=xq_scales[:, cols], start=True, stop=True)
+                h_banks.append((h[t][:, cols], bank))
+        for rows, bank in h_banks:
+            nc.scalar.activation(out=rows, in_=bank[:], func=ACT.Relu)
 
-        ww = keep.tile([P, 3, 2 * N], U8, name="ww", tag="w1_raw2", align_bytes=64)
+        ww = keep.tile([P, 3, 2 * N], U8, name="ww", tag="w1_raw1", align_bytes=64)
         for w in range(3):
             nc.scalar.copy(ww[:, w, :].bitcast(U16).rearrange("p (t m) -> p t m", t=PACK),
                            ww_raw[w][:].bitcast(U16).rearrange("p (m t) -> p t m", t=PACK))
@@ -230,28 +234,28 @@ def tile_picked_zmix_none_po_kernel(
         def out_banks(half):
             return [acc.tile([P, 2, HALF], F32, name="bank%d" % (2 * half + u)) for u in range(2)]
 
-        plain_near = fetch_plain(near, (0, 0, 1, 1))
+        plain_near = fetch_plain(near, (0, 0, 0, 1))
         terms_near = ring.tile([P, PACK, D, V], F32, name="terms")
-        weigh(terms_near, plain_near, near, gate_near, WHOLE, (0, 0, 1, 1))
+        weigh(terms_near, plain_near, near, gate_near, WHOLE, (0, 0, 0, 1))
         total_a1, total_b1 = add_turned(terms_near, (0, 1))
-        plain_far = fetch_plain(far, (2, 2, 2, 1))
+        plain_far = fetch_plain(far, (2, 2, 2, 2))
         terms_far = ring.tile([P, PACK, D, V], F32, name="terms")
         back_a1 = turn_back(total_a1)
         back_b1 = turn_back(total_b1)
         banks_a = out_banks(0)
         banks_b = out_banks(1)
         z_a1 = weave_back(back_a1)
-        weigh(terms_far, plain_far, far, gate_far, HALVES[0], (2, 2, 2, 1))
+        weigh(terms_far, plain_far, far, gate_far, HALVES[0], (2, 2, 2, 2))
         total_a2, = add_turned(terms_far, (0,))
         gather_own(HALVES[0], 4)
         z_b1 = weave_back(back_b1)
         multiply(z_a1, 0, banks_a, True, False)
         back_a2 = turn_back(total_a2)
-        z_a0 = weave(nc.scalar.copy, own[:, :, HALVES[0]], "z")
+        z_a0 = weave(nc.vector.tensor_copy, own[:, :, HALVES[0]], "z")
         z_a2 = weave_back(back_a2)
-        gather_own(HALVES[1], 2)
+        gather_own(HALVES[1], 4)
         multiply(z_b1, 0, banks_b, True, False)
-        z_b2 = weigh_and_add(terms_far, plain_far, far, gate_far, HALVES[1], (2, 2, 2, 1), lambda: [multiply(z_a0, 2, banks_a, False, False), multiply(z_a2, 1, banks_a, False, True)])
+        z_b2 = weigh_and_add(terms_far, plain_far, far, gate_far, HALVES[1], (2, 2, 2, 2), lambda: [multiply(z_a0, 2, banks_a, False, False), multiply(z_a2, 1, banks_a, False, True)])
         multiply(weave(nc.vector.tensor_copy, own[:, :, HALVES[1]], "z"), 2, banks_b, False, False)
         multiply(z_b2, 1, banks_b, False, True)
         hand_out(banks_a, 0, False)

@@ -19,10 +19,17 @@ ALU = mybir.AluOpType
 
 P = 128
 PACK = 4
-HALF = 128
-HALVES = (slice(0, HALF), slice(HALF, V))
-WHOLE = slice(0, V)
-W1_PARTS = ((0, 64), (64, 128))
+QUADRANTS = 4
+SCALE_ROWS = 16
+LIST_ROWS = 16
+HALF = V // 2
+FIRST, LAST, BOTH = slice(0, HALF), slice(HALF, V), slice(0, V)
+NEAR, FAR, OWN = 0, 1, 2
+RUN = 4
+PARTS = 2 * 3
+W1_HALF = P // 2
+W1_SPLIT = 86
+FAR_ON_SCALAR = 2
 
 
 def tile_picked_zmix_none_po_kernel(
@@ -34,23 +41,12 @@ def tile_picked_zmix_none_po_kernel(
         keep = ctx.enter_context(tc.tile_pool(name="keep", bufs=1))
         ring = ctx.enter_context(tc.tile_pool(name="ring", bufs=2))
         acc = ctx.enter_context(tc.psum_pool(name="acc", bufs=1))
-        turn = ctx.enter_context(tc.psum_pool(name="turn", bufs=2))
+        turn = ctx.enter_context(tc.psum_pool(name="turn", bufs=3))
 
         def load_list(name, source):
             tile = keep.tile(list(source.shape), U16, name=name)
             nc.sync.dma_start(tile[:], source)
             return tile
-
-        xs = keep.tile([P, T], U8, name="xs", align_bytes=64)
-        nc.gpsimd.memset(xs[:].bitcast(I32), 0)
-        ws_raw = keep.tile([P, N], U8, name="ws_raw", align_bytes=64)
-        nc.gpsimd.memset(ws_raw[:].bitcast(I32), 0)
-        for w, source in enumerate((w3_scales, w4_scales, w2_scales)):
-            nc.gpsimd.dma_start(ws_raw[16 * w : 16 * (w + 1), :].bitcast(I32), source[0].bitcast(I32))
-        ws = keep.tile([P, 3, N], U8, name="ws", align_bytes=64)
-        nc.gpsimd.memset(ws[:].rearrange("p w n -> p (w n)").bitcast(I32), 0)
-        ident = keep.tile([P, P], F32, name="ident")
-        make_identity(nc, ident[:])
 
         def load_gate(name, source):
             tile = keep.tile([P, D, V], F32, name=name)
@@ -62,204 +58,228 @@ def tile_picked_zmix_none_po_kernel(
             nc.sync.dma_start(tile[:].bitcast(I32), source[0].bitcast(I32))
             return tile
 
-        offs_t = load_list("offs_t", offs)
-        for q in range(4):
-            (nc.sync if q < 2 else nc.scalar).dma_start(xs[32 * q : 32 * q + 4, :].bitcast(I32), x_scales[0, 4 * q : 4 * q + 4, :].bitcast(I32))
-        xw = keep.tile([P, T], U32, name="xw", align_bytes=64)
-        nc.sync.dma_start(xw[:].bitcast(I32), x_words[0].rearrange("p n t -> p (n t)").bitcast(I32))
+        def scale_rows(q):
+            return slice(PACK * q, PACK * (q + 1)), slice(32 * q, 32 * q + PACK)
+
+        x_scale_table = keep.tile([P, T], U8, name="x_scale_table", align_bytes=64)
+        nc.gpsimd.memset(x_scale_table[:].bitcast(I32), 0)
+        w_scales_raw = keep.tile([P, N], U8, name="w_scales_raw", align_bytes=64)
+        nc.gpsimd.memset(w_scales_raw[:].bitcast(I32), 0)
+        for w, source in ((NEAR, w3_scales), (FAR, w4_scales), (OWN, w2_scales)):
+            nc.gpsimd.dma_start(w_scales_raw[SCALE_ROWS * w : SCALE_ROWS * (w + 1), :].bitcast(I32), source[0].bitcast(I32))
+        w_scales = keep.tile([P, 3, N], U8, name="w_scales", align_bytes=64)
+        nc.gpsimd.memset(w_scales[:].rearrange("p w n -> p (w n)").bitcast(I32), 0)
+        identity = keep.tile([P, P], F32, name="identity")
+        make_identity(nc, identity[:])
+
+        offs_list = load_list("offs_list", offs)
+        x_word_table = keep.tile([P, T], U32, name="x_word_table", align_bytes=64)
+        nc.sync.dma_start(x_word_table[:].bitcast(I32), x_words[0].rearrange("p n t -> p (n t)").bitcast(I32))
+        for q in range(QUADRANTS):
+            rows, partitions = scale_rows(q)
+            queue = nc.sync if q < QUADRANTS // 2 else nc.scalar
+            queue.dma_start(x_scale_table[partitions, :].bitcast(I32), x_scales[0, rows, :].bitcast(I32))
         w1_rows = w1.rearrange("(p j) c -> p j c", j=PACK)
         w1_raw = []
-        for q, (m0, m1) in enumerate(W1_PARTS):
-            part = keep.tile([P, PACK, PACK * (m1 - m0)], F32, name="w1_raw%d" % q, align_bytes=64)
-            nc.sync.dma_start(part[:], w1_rows[:, :, PACK * m0 : PACK * m1])
-            w1_raw.append(part)
-        near = [load_list("pos%d_t" % d, source) for d, source in enumerate((pos1, pos2, pos3))]
-        ww_raw = [load_words("w%d_raw" % w, source) for w, source in enumerate((w3_words, w4_words, w2_words))]
+        for part in range(2):
+            tile = keep.tile([P, PACK, PACK * W1_HALF], F32, name="w1_raw%d" % part, align_bytes=64)
+            nc.sync.dma_start(tile[:], w1_rows[:, :, PACK * W1_HALF * part : PACK * W1_HALF * (part + 1)])
+            w1_raw.append(tile)
+        w_words_raw = [load_words("w3_raw", w3_words), load_words("w4_raw", w4_words)]
+        near = [load_list("near%d_list" % d, source) for d, source in enumerate((pos1, pos2, pos3))]
         gate_near = load_gate("gate_near", gate)
-        far = [load_list("far%d_t" % d, source) for d, source in enumerate((far1, far2, far3))]
+        w_words_raw.append(load_words("w2_raw", w2_words))
+        far = [load_list("far%d_list" % d, source) for d, source in enumerate((far1, far2, far3))]
         gate_far = load_gate("gate_far", gate2)
-        cen_t = load_list("cen_t", cen)
+        cen_list = load_list("cen_list", cen)
 
-        xq_words = keep.tile([P, S], U32, name="xq_words", align_bytes=64)
-        nc.vector.tensor_copy(xq_words[:], xw[:].indirect(offs_t[:]))
-        xq_scales = keep.tile([P, S], U8, name="xq_scales", align_bytes=64)
-        nc.vector.tensor_copy(xq_scales[:], xs[:].indirect(offs_t[:]))
+        picked_words = keep.tile([P, S], U32, name="picked_words", align_bytes=64)
+        nc.vector.tensor_copy(picked_words[:], x_word_table[:].indirect(offs_list[:]))
+        picked_scales = keep.tile([P, S], U8, name="picked_scales", align_bytes=64)
+        nc.vector.tensor_copy(picked_scales[:], x_scale_table[:].indirect(offs_list[:]))
 
-        w1_bf = keep.tile([P, PACK, P, PACK], BF16, name="w1_bf", tag="dealt", align_bytes=64)
+        w1_bf = keep.tile([P, PACK, P, PACK], BF16, name="w1_bf", tag="dealing", align_bytes=64)
 
-        def deal_w1(q, m0, m1, on_scalar):
-            first = W1_PARTS[q][0]
-            dst = w1_bf[:, :, m0:m1, :].rearrange("p t m j -> p m j t")
-            src = w1_raw[q][:, :, PACK * (m0 - first) : PACK * (m1 - first)].rearrange("p j (m t) -> p m j t", t=PACK)
-            if on_scalar:
-                nc.scalar.activation(out=dst, in_=src, func=ACT.Copy)
-            else:
-                nc.vector.tensor_copy(dst, src)
+        def w1_views(m0, m1):
+            part, local = divmod(m0, W1_HALF)
+            source = w1_raw[part][:, :, PACK * local : PACK * (local + m1 - m0)]
+            return w1_bf[:, :, m0:m1, :].rearrange("p t m j -> p m j t"), source.rearrange("p j (m t) -> p m j t", t=PACK)
 
-        deal_w1(0, 0, 64, True)
-        deal_w1(1, 64, 86, True)
-        deal_w1(1, 86, 128, False)
+        nc.scalar.activation(*w1_views(0, W1_HALF), ACT.Copy)
+        nc.scalar.activation(*w1_views(W1_HALF, W1_SPLIT), ACT.Copy)
+        nc.vector.tensor_copy(*w1_views(W1_SPLIT, P))
+
         h = []
-        h_banks = []
+        to_relu = []
         for t in range(PACK):
-            codes = keep.tile([P, P], U32, name="w1_codes%d" % t, align_bytes=64)
-            scales = keep.tile([P, P], U8, name="w1_scales%d" % t, align_bytes=64)
-            nc.vector.quantize_mx(out=codes[:].bitcast(FP8X4), scales=scales[:], in_=w1_bf[:, t].rearrange("p m j -> p (m j)"))
+            w1_codes = keep.tile([P, P], U32, name="w1_codes%d" % t, align_bytes=64)
+            w1_scales = keep.tile([P, P], U8, name="w1_scales%d" % t, align_bytes=64)
+            nc.vector.quantize_mx(out=w1_codes[:].bitcast(FP8X4), scales=w1_scales[:], in_=w1_bf[:, t].rearrange("p m j -> p (m j)"))
             h.append(keep.tile([P, S], F32, name="h%d" % t))
             if t == 0:
-                parts = [(turn.tile([P, S // 2], F32, name="back", bufs=2), slice(0, S // 2)), (acc.tile([P, S // 2], F32, name="bank0"), slice(S // 2, S))]
+                pieces = [(turn.tile([P, S // 2], F32, name="back"), slice(0, S // 2)),
+                          (acc.tile([P, S // 2], F32, name="bank0"), slice(S // 2, S))]
             else:
-                parts = [(acc.tile([P, S], F32, name="bank%d" % t), slice(0, S))]
-            for bank, cols in parts:
-                nc.tensor.matmul_mx(out=bank[:], lhsT=codes[:].bitcast(FP8X4), lhsT_scale=scales[:],
-                                    rhs=xq_words[:, cols].bitcast(FP8X4), rhs_scale=xq_scales[:, cols], start=True, stop=True)
-                h_banks.append((h[t][:, cols], bank))
-        for rows, bank in h_banks:
+                pieces = [(acc.tile([P, S], F32, name="bank%d" % t), slice(0, S))]
+            for bank, entries in pieces:
+                nc.tensor.matmul_mx(out=bank[:], lhsT=w1_codes[:].bitcast(FP8X4), lhsT_scale=w1_scales[:],
+                                    rhs=picked_words[:, entries].bitcast(FP8X4), rhs_scale=picked_scales[:, entries],
+                                    start=True, stop=True)
+                to_relu.append((h[t][:, entries], bank))
+        for rows, bank in to_relu:
             nc.scalar.activation(out=rows, in_=bank[:], func=ACT.Relu)
 
-        ww = keep.tile([P, 3, 2 * N], U8, name="ww", tag="w1_raw1", align_bytes=64)
-        for w in range(3):
-            nc.scalar.copy(ww[:, w, :].bitcast(U16).rearrange("p (t m) -> p t m", t=PACK),
-                           ww_raw[w][:].bitcast(U16).rearrange("p (m t) -> p t m", t=PACK))
-        ws_dealt = keep.tile([P, N], U8, name="ws_dealt", tag="dealt", align_bytes=64)
-        nc.vector.tensor_copy(ws_dealt[:].rearrange("p (t m) -> p t m", t=PACK), ws_raw[:].rearrange("p (m t) -> p t m", t=PACK))
-        for w in range(3):
-            for q in range(4):
-                row = 16 * w + 4 * q
-                nc.sync.dma_start(ws[32 * q : 32 * q + 4, w, :].bitcast(I32), ws_dealt[row : row + 4, :].bitcast(I32))
+        w_words = keep.tile([P, 3, 2 * N], U8, name="w_words", tag="w1_raw1", align_bytes=64)
+        for w in (NEAR, FAR, OWN):
+            nc.scalar.copy(w_words[:, w, :].bitcast(U16).rearrange("p (t m) -> p t m", t=PACK),
+                           w_words_raw[w][:].bitcast(U16).rearrange("p (m t) -> p t m", t=PACK))
+        w_scales_dealt = keep.tile([P, N], U8, name="w_scales_dealt", tag="dealing", align_bytes=64)
+        nc.vector.tensor_copy(w_scales_dealt[:].rearrange("p (t m) -> p t m", t=PACK),
+                              w_scales_raw[:].rearrange("p (m t) -> p t m", t=PACK))
+        for w in (NEAR, FAR, OWN):
+            dealt_rows = w_scales_dealt[SCALE_ROWS * w : SCALE_ROWS * (w + 1), :]
+            for q in range(QUADRANTS):
+                rows, partitions = scale_rows(q)
+                nc.sync.dma_start(w_scales[partitions, w, :].bitcast(I32), dealt_rows[rows, :].bitcast(I32))
 
         y_words = keep.tile([P, V], U32, name="y_words", align_bytes=64)
         y_scales = keep.tile([P, V], U8, name="y_scales", align_bytes=64)
         out_rows = out_0.rearrange("(p t) v -> p t v", t=PACK)
-        out_words = out_1[0].rearrange("p v t -> p (v t)").bitcast(I32)
-
         own = keep.tile([P, PACK, V], BF16, name="own")
 
-        def offsets(tile, cols):
-            return tile[:, cols.start // 16 : cols.stop // 16]
+        def looked_up(t, entries, cols):
+            return h[t][:].indirect(entries[:, cols.start // LIST_ROWS : cols.stop // LIST_ROWS])
 
-        def fetch_plain(lists, counts):
-            plain = ring.tile([P, PACK, D, V], F32, name="plain")
-            for t in range(PACK):
-                for d in range(D - counts[t], D):
-                    nc.scalar.activation(out=plain[:, t, d, :], in_=h[t][:].indirect(lists[d][:]), func=ACT.Copy)
-            return plain
+        def fetch(out, t, entries, cols):
+            nc.scalar.activation(out=out, in_=looked_up(t, entries, cols), func=ACT.Copy)
 
-        def weigh_plain(terms, plain, gates, cols, t, count):
-            if count:
-                nc.vector.tensor_tensor(terms[:, t, D - count :, cols], plain[:, t, D - count :, cols], gates[:, D - count :, cols], ALU.mult)
+        def fetch_weighed(terms, lists, gates, t, d, cols):
+            nc.vector.tensor_tensor(terms[:, t, d, cols], looked_up(t, lists[d], cols), gates[:, d, cols], ALU.mult)
 
-        def fetch_weighed(terms, lists, gates, cols, t, d):
-            nc.vector.tensor_tensor(terms[:, t, d, cols], h[t][:].indirect(offsets(lists[d], cols)), gates[:, d, cols], ALU.mult)
+        def weigh(terms, fetched, gates, t, first, cols):
+            nc.vector.tensor_tensor(terms[:, t, first:, cols], fetched[:, t, first:, cols], gates[:, first:, cols], ALU.mult)
 
-        def weigh(terms, plain, lists, gates, cols, counts):
-            for t in range(PACK):
-                for d in range(D - counts[t]):
-                    fetch_weighed(terms, lists, gates, cols, t, d)
-                weigh_plain(terms, plain, gates, cols, t, counts[t])
-
-        def add_turned(terms, halves):
-            totals = [turn.tile([P, PACK, P], F32, name="total", bufs=2) for half in halves]
-            for t in range(PACK):
-                for total, half in zip(totals, halves):
-                    for d in range(D):
-                        nc.tensor.matmul(total[:, t, :], lhsT=terms[:, t, d, HALVES[half]], rhs=ident[:], is_transpose=True,
-                                         start=(d == 0), stop=(d == D - 1))
-            return totals
-
-        def weigh_and_add(terms, plain, lists, gates, cols, counts, between):
-            two = ring.tile([P, PACK, HALF], F32, name="two")
-            for t in range(PACK):
-                weigh_plain(terms, plain, gates, cols, t, counts[t])
-            for d in reversed(range(D)):
-                for t in range(PACK):
-                    if d < D - counts[t]:
-                        fetch_weighed(terms, lists, gates, cols, t, d)
-                    if d == 0 and t == 0:
-                        nc.vector.tensor_tensor(two[:], terms[:, :, 1, cols], terms[:, :, 2, cols], ALU.add)
-            between()
-            z = ring.tile([P, HALF * PACK], BF16, name="z", align_bytes=64, bufs=6)
-            nc.vector.tensor_tensor(z[:].rearrange("p (c i t) -> p c t i", i=4, t=PACK), terms[:, :, 0, cols].rearrange("p t (c i) -> p c t i", i=4),
-                                    two[:].rearrange("p t (c i) -> p c t i", i=4), ALU.add)
-            return z
+        def add_turned(total, terms, t, cols):
+            for d in range(D):
+                nc.tensor.matmul(total[:, t, :], lhsT=terms[:, t, d, cols], rhs=identity[:], is_transpose=True,
+                                 start=(d == 0), stop=(d == D - 1))
 
         def turn_back(total):
             pairs = ring.tile([P, 2, P, 2], BF16, name="pairs", bufs=3)
             nc.scalar.activation(out=pairs[:], in_=total[:].rearrange("v (u e) p -> v u p e", e=2), func=ACT.Copy)
             words = pairs[:].rearrange("v u p e -> v u (p e)").bitcast(F32)
-            back = turn.tile([P, 2, HALF], F32, name="back", bufs=2)
+            back = turn.tile([P, 2, HALF], F32, name="back")
             for u in range(2):
-                nc.tensor.transpose(back[:, u, :], words[:, u, :], ident[:])
+                nc.tensor.transpose(back[:, u, :], words[:, u, :], identity[:])
             return back
 
+        def woven_tile(name, bufs):
+            return ring.tile([P, HALF * PACK], BF16, name=name, align_bytes=64, bufs=bufs)
+
+        def by_runs(tiles):
+            return tiles.rearrange("p t (c i) -> p c t i", i=RUN)
+
+        def woven_by_runs(woven):
+            return woven[:].rearrange("p (c i t) -> p c t i", i=RUN, t=PACK)
+
         def weave_back(back):
-            z = ring.tile([P, HALF * PACK], BF16, name="z", align_bytes=64, bufs=6)
+            z = woven_tile("z", PARTS)
             nc.scalar.copy(z[:].bitcast(F32).rearrange("p (v u) -> p v u", u=2), back[:].rearrange("p u v -> p v u"))
             return z
 
-        def gather_own(cols, on_scalar):
+        def weave_own(cols):
+            z = woven_tile("z", PARTS)
+            nc.vector.tensor_copy(woven_by_runs(z), by_runs(own[:, :, cols]))
+            return z
+
+        def multiply(z, w, banks, opens=False, closes=False):
+            z_codes = ring.tile([P, HALF], U32, name="z_codes", align_bytes=64, bufs=PARTS)
+            z_scales = ring.tile([P, HALF], U8, name="z_scales", align_bytes=64, bufs=PARTS)
+            nc.vector.quantize_mx(out=z_codes[:].bitcast(FP8X4), scales=z_scales[:], in_=z[:])
             for t in range(PACK):
-                if t < on_scalar:
-                    nc.scalar.activation(out=own[:, t, cols], in_=h[t][:].indirect(offsets(cen_t, cols)), func=ACT.Copy)
-                else:
-                    nc.vector.tensor_copy(own[:, t, cols], h[t][:].indirect(offsets(cen_t, cols)))
+                u, e = divmod(t, 2)
+                nc.tensor.matmul_mx(out=banks[u][:, e, :], lhsT=w_words[:, w, 2 * P * t : 2 * P * (t + 1)].bitcast(FP4X4),
+                                    lhsT_scale=w_scales[:, w, P * t : P * (t + 1)],
+                                    rhs=z_codes[:].bitcast(FP8X4), rhs_scale=z_scales[:],
+                                    start=(opens and e == 0), stop=(closes and e == 1))
 
-        def weave(copy, source, name):
-            woven = ring.tile([P, HALF * PACK], BF16, name=name, align_bytes=64, bufs=6)
-            copy(woven[:].rearrange("p (c i t) -> p c t i", i=4, t=PACK), source.rearrange("p t (c i) -> p c t i", i=4))
-            return woven
-
-        def multiply(z, w, banks, first, last):
-            codes = ring.tile([P, HALF], U32, name="z_codes", align_bytes=64, bufs=6)
-            scales = ring.tile([P, HALF], U8, name="z_scales", align_bytes=64, bufs=6)
-            nc.vector.quantize_mx(out=codes[:].bitcast(FP8X4), scales=scales[:], in_=z[:])
-            for t in range(PACK):
-                nc.tensor.matmul_mx(out=banks[t // 2][:, t % 2, :], lhsT=ww[:, w, 2 * P * t : 2 * P * (t + 1)].bitcast(FP4X4),
-                                    lhsT_scale=ws[:, w, P * t : P * (t + 1)], rhs=codes[:].bitcast(FP8X4), rhs_scale=scales[:],
-                                    start=(first and t % 2 == 0), stop=(last and t % 2 == 1))
-
-        def hand_out(banks, half, both):
-            cols = slice(half * HALF, (half + 1) * HALF)
-            y = ring.tile([P, PACK, HALF], F32, name="y")
-            nc.scalar.copy(y[:, 0:2, :], banks[0][:])
-            if both:
-                nc.vector.tensor_copy(y[:, 2:4, :], banks[1][:])
-            else:
-                nc.scalar.copy(y[:, 2:4, :], banks[1][:])
-            nc.sync.dma_start(out_rows[:, :, cols], y[:])
-            y_bf = weave(nc.vector.tensor_copy if both or not False else nc.scalar.copy, y[:], "y_bf")
+        def quantise_y(y_bf, cols):
             nc.vector.quantize_mx(out=y_words[:, cols].bitcast(FP8X4), scales=y_scales[:, cols], in_=y_bf[:])
-            nc.sync.dma_start(out_words[:, cols], y_words[:, cols].bitcast(I32))
 
-        def out_banks(half):
-            return [acc.tile([P, 2, HALF], F32, name="bank%d" % (2 * half + u)) for u in range(2)]
-
-        plain_near = fetch_plain(near, (0, 0, 0, 1))
+        fetched_near = ring.tile([P, PACK, D, V], F32, name="fetched")
+        fetch(fetched_near[:, PACK - 1, D - 1, :], PACK - 1, near[D - 1], BOTH)
         terms_near = ring.tile([P, PACK, D, V], F32, name="terms")
-        weigh(terms_near, plain_near, near, gate_near, WHOLE, (0, 0, 0, 1))
-        total_a1, total_b1 = add_turned(terms_near, (0, 1))
-        plain_far = fetch_plain(far, (2, 2, 2, 2))
+        for t in range(PACK):
+            for d in range(D if t < PACK - 1 else D - 1):
+                fetch_weighed(terms_near, near, gate_near, t, d, BOTH)
+        weigh(terms_near, fetched_near, gate_near, PACK - 1, D - 1, BOTH)
+        near_first, near_last = [acc.tile([P, PACK, P], F32, name="bank%d" % u) for u in range(2)]
+        for t in range(PACK):
+            add_turned(near_first, terms_near, t, FIRST)
+            add_turned(near_last, terms_near, t, LAST)
+
+        far_first_on_scalar = D - FAR_ON_SCALAR
+        fetched_far = ring.tile([P, PACK, D, V], F32, name="fetched")
+        for t in range(PACK):
+            for d in range(far_first_on_scalar, D):
+                fetch(fetched_far[:, t, d, :], t, far[d], BOTH)
         terms_far = ring.tile([P, PACK, D, V], F32, name="terms")
-        back_a1 = turn_back(total_a1)
-        back_b1 = turn_back(total_b1)
-        banks_a = out_banks(0)
-        banks_b = out_banks(1)
-        z_a1 = weave_back(back_a1)
-        weigh(terms_far, plain_far, far, gate_far, HALVES[0], (2, 2, 2, 2))
-        total_a2, = add_turned(terms_far, (0,))
-        gather_own(HALVES[0], 4)
-        z_b1 = weave_back(back_b1)
-        multiply(z_a1, 0, banks_a, True, False)
-        back_a2 = turn_back(total_a2)
-        z_a0 = weave(nc.vector.tensor_copy, own[:, :, HALVES[0]], "z")
-        z_a2 = weave_back(back_a2)
-        gather_own(HALVES[1], 4)
-        multiply(z_b1, 0, banks_b, True, False)
-        z_b2 = weigh_and_add(terms_far, plain_far, far, gate_far, HALVES[1], (2, 2, 2, 2), lambda: [multiply(z_a0, 2, banks_a, False, False), multiply(z_a2, 1, banks_a, False, True)])
-        multiply(weave(nc.vector.tensor_copy, own[:, :, HALVES[1]], "z"), 2, banks_b, False, False)
-        multiply(z_b2, 1, banks_b, False, True)
-        hand_out(banks_a, 0, False)
-        hand_out(banks_b, 1, True)
-        for q in range(4):
-            queue = nc.sync if q % 2 == 0 else nc.scalar
-            queue.dma_start(out_2[0, 4 * q : 4 * q + 4, :].bitcast(I32), y_scales[32 * q : 32 * q + 4, :].bitcast(I32))
+        banks_first = [acc.tile([P, 2, HALF], F32, name="bank%d" % (2 + u)) for u in range(2)]
+        banks_last = [acc.tile([P, 2, HALF], F32, name="bank%d" % u) for u in range(2)]
+        for t in range(PACK):
+            fetch(own[:, t, FIRST], t, cen_list, FIRST)
+        back_first = turn_back(near_first)
+        back_last = turn_back(near_last)
+        multiply(weave_back(back_first), NEAR, banks_first, opens=True)
+        multiply(weave_back(back_last), NEAR, banks_last, opens=True)
+
+        for t in range(PACK):
+            for d in range(far_first_on_scalar):
+                fetch_weighed(terms_far, far, gate_far, t, d, FIRST)
+            weigh(terms_far, fetched_far, gate_far, t, far_first_on_scalar, FIRST)
+        far_first = turn.tile([P, PACK, P], F32, name="far_first", bufs=1)
+        for t in range(PACK):
+            add_turned(far_first, terms_far, t, FIRST)
+        z2_first = weave_back(turn_back(far_first))
+        for t in range(PACK):
+            fetch(own[:, t, LAST], t, cen_list, LAST)
+
+        two_terms = ring.tile([P, PACK, HALF], F32, name="two_terms")
+        for t in range(PACK):
+            weigh(terms_far, fetched_far, gate_far, t, far_first_on_scalar, LAST)
+        for t in range(PACK):
+            fetch_weighed(terms_far, far, gate_far, t, 0, LAST)
+            if t == 0:
+                nc.vector.tensor_tensor(two_terms[:], terms_far[:, :, 1, LAST], terms_far[:, :, 2, LAST], ALU.add)
+        multiply(weave_own(FIRST), OWN, banks_first)
+        multiply(z2_first, FAR, banks_first, closes=True)
+        z2_last = woven_tile("z", PARTS)
+        nc.vector.tensor_tensor(woven_by_runs(z2_last), by_runs(terms_far[:, :, 0, LAST]), by_runs(two_terms[:]), ALU.add)
+        multiply(weave_own(LAST), OWN, banks_last)
+        multiply(z2_last, FAR, banks_last, closes=True)
+
+        y_first = ring.tile([P, PACK, HALF], F32, name="y")
+        for u in range(2):
+            nc.scalar.copy(y_first[:, 2 * u : 2 * u + 2, :], banks_first[u][:])
+        nc.sync.dma_start(out_rows[:, :, FIRST], y_first[:])
+        y_first_bf = woven_tile("y_bf", 2)
+        nc.vector.tensor_copy(woven_by_runs(y_first_bf), by_runs(y_first[:]))
+        quantise_y(y_first_bf, FIRST)
+
+        y_last_bf = woven_tile("y_bf", 2)
+        y_pairs = y_last_bf[:].rearrange("p (v u e) -> p u v e", u=2, e=2)
+        y_last = ring.tile([P, PACK, HALF], F32, name="y")
+        copies = (nc.scalar.copy, nc.vector.tensor_copy)
+        for u in range(2):
+            copies[u](y_pairs[:, u], banks_last[u][:].rearrange("p e v -> p v e"))
+        for u in range(2):
+            copies[u](y_last[:, 2 * u : 2 * u + 2, :], banks_last[u][:])
+        for u, queue in enumerate((nc.scalar, nc.sync)):
+            queue.dma_start(out_rows[:, 2 * u : 2 * u + 2, LAST], y_last[:, 2 * u : 2 * u + 2, :])
+        quantise_y(y_last_bf, LAST)
+
+        nc.scalar.dma_start(out_1[0].rearrange("p v t -> p (v t)").bitcast(I32), y_words[:].bitcast(I32))
+        for q in range(QUADRANTS):
+            rows, partitions = scale_rows(q)
+            queue = nc.sync if q < QUADRANTS - 1 else nc.scalar
+            queue.dma_start(out_2[0, rows, :].bitcast(I32), y_scales[partitions, :].bitcast(I32))

from contextlib import ExitStack

import concourse.mybir as mybir
from concourse.masks import make_identity

K, T, S, D, V, H, N = 512, 1024, 512, 3, 256, 512, 512
FLOPS = 2 * K * H * S + 3 * 2 * H * N * V

F32 = mybir.dt.float32
BF16 = mybir.dt.bfloat16
I32 = mybir.dt.int32
U32 = mybir.dt.uint32
U16 = mybir.dt.uint16
U8 = mybir.dt.uint8
FP8X4 = mybir.dt.float8_e4m3fn_x4
FP4X4 = mybir.dt.float4_e2m1fn_x4
ACT = mybir.ActivationFunctionType
ALU = mybir.AluOpType

P = 128
PACK = 4
QUADRANTS = 4
SCALE_ROWS = 16
LIST_ROWS = 16
HALF = V // 2
FIRST, LAST, BOTH = slice(0, HALF), slice(HALF, V), slice(0, V)
NEAR, FAR, OWN = 0, 1, 2
RUN = 4
PARTS = 2 * 3
W1_HALF = P // 2
W1_SPLIT = 86
FAR_ON_SCALAR = 2


def tile_picked_zmix_none_po_kernel(
    tc, x_words, x_scales, w1, w2_words, w2_scales, w3_words, w3_scales, w4_words, w4_scales,
    gate, gate2, offs, cen, pos1, pos2, pos3, far1, far2, far3, out_0, out_1, out_2,
):
    nc = tc.nc
    with ExitStack() as ctx:
        keep = ctx.enter_context(tc.tile_pool(name="keep", bufs=1))
        ring = ctx.enter_context(tc.tile_pool(name="ring", bufs=2))
        acc = ctx.enter_context(tc.psum_pool(name="acc", bufs=1))
        turn = ctx.enter_context(tc.psum_pool(name="turn", bufs=3))

        def load_list(name, source):
            tile = keep.tile(list(source.shape), U16, name=name)
            nc.sync.dma_start(tile[:], source)
            return tile

        def load_gate(name, source):
            tile = keep.tile([P, D, V], F32, name=name)
            nc.sync.dma_start(tile[:], source.rearrange("d p v -> p d v"))
            return tile

        def load_words(name, source):
            tile = keep.tile([P, 2 * N], U8, name=name, align_bytes=64)
            nc.sync.dma_start(tile[:].bitcast(I32), source[0].bitcast(I32))
            return tile

        def scale_rows(q):
            return slice(PACK * q, PACK * (q + 1)), slice(32 * q, 32 * q + PACK)

        x_scale_table = keep.tile([P, T], U8, name="x_scale_table", align_bytes=64)
        nc.gpsimd.memset(x_scale_table[:].bitcast(I32), 0)
        w_scales_raw = keep.tile([P, N], U8, name="w_scales_raw", align_bytes=64)
        nc.gpsimd.memset(w_scales_raw[:].bitcast(I32), 0)
        for w, source in ((NEAR, w3_scales), (FAR, w4_scales), (OWN, w2_scales)):
            nc.gpsimd.dma_start(w_scales_raw[SCALE_ROWS * w : SCALE_ROWS * (w + 1), :].bitcast(I32), source[0].bitcast(I32))
        w_scales = keep.tile([P, 3, N], U8, name="w_scales", align_bytes=64)
        nc.gpsimd.memset(w_scales[:].rearrange("p w n -> p (w n)").bitcast(I32), 0)
        identity = keep.tile([P, P], F32, name="identity")
        make_identity(nc, identity[:])

        offs_list = load_list("offs_list", offs)
        x_word_table = keep.tile([P, T], U32, name="x_word_table", align_bytes=64)
        nc.sync.dma_start(x_word_table[:].bitcast(I32), x_words[0].rearrange("p n t -> p (n t)").bitcast(I32))
        for q in range(QUADRANTS):
            rows, partitions = scale_rows(q)
            queue = nc.sync if q < QUADRANTS // 2 else nc.scalar
            queue.dma_start(x_scale_table[partitions, :].bitcast(I32), x_scales[0, rows, :].bitcast(I32))
        w1_rows = w1.rearrange("(p j) c -> p j c", j=PACK)
        w1_raw = []
        for part in range(2):
            tile = keep.tile([P, PACK, PACK * W1_HALF], F32, name="w1_raw%d" % part, align_bytes=64)
            nc.sync.dma_start(tile[:], w1_rows[:, :, PACK * W1_HALF * part : PACK * W1_HALF * (part + 1)])
            w1_raw.append(tile)
        w_words_raw = [load_words("w3_raw", w3_words), load_words("w4_raw", w4_words)]
        near = [load_list("near%d_list" % d, source) for d, source in enumerate((pos1, pos2, pos3))]
        gate_near = load_gate("gate_near", gate)
        w_words_raw.append(load_words("w2_raw", w2_words))
        far = [load_list("far%d_list" % d, source) for d, source in enumerate((far1, far2, far3))]
        gate_far = load_gate("gate_far", gate2)
        cen_list = load_list("cen_list", cen)

        picked_words = keep.tile([P, S], U32, name="picked_words", align_bytes=64)
        nc.vector.tensor_copy(picked_words[:], x_word_table[:].indirect(offs_list[:]))
        picked_scales = keep.tile([P, S], U8, name="picked_scales", align_bytes=64)
        nc.vector.tensor_copy(picked_scales[:], x_scale_table[:].indirect(offs_list[:]))

        w1_bf = keep.tile([P, PACK, P, PACK], BF16, name="w1_bf", tag="dealing", align_bytes=64)

        def w1_views(m0, m1):
            part, local = divmod(m0, W1_HALF)
            source = w1_raw[part][:, :, PACK * local : PACK * (local + m1 - m0)]
            return w1_bf[:, :, m0:m1, :].rearrange("p t m j -> p m j t"), source.rearrange("p j (m t) -> p m j t", t=PACK)

        nc.scalar.activation(*w1_views(0, W1_HALF), ACT.Copy)
        nc.scalar.activation(*w1_views(W1_HALF, W1_SPLIT), ACT.Copy)
        nc.vector.tensor_copy(*w1_views(W1_SPLIT, P))

        h = []
        to_relu = []
        for t in range(PACK):
            w1_codes = keep.tile([P, P], U32, name="w1_codes%d" % t, align_bytes=64)
            w1_scales = keep.tile([P, P], U8, name="w1_scales%d" % t, align_bytes=64)
            nc.vector.quantize_mx(out=w1_codes[:].bitcast(FP8X4), scales=w1_scales[:], in_=w1_bf[:, t].rearrange("p m j -> p (m j)"))
            h.append(keep.tile([P, S], F32, name="h%d" % t))
            if t == 0:
                pieces = [(turn.tile([P, S // 2], F32, name="back"), slice(0, S // 2)),
                          (acc.tile([P, S // 2], F32, name="bank0"), slice(S // 2, S))]
            else:
                pieces = [(acc.tile([P, S], F32, name="bank%d" % t), slice(0, S))]
            for bank, entries in pieces:
                nc.tensor.matmul_mx(out=bank[:], lhsT=w1_codes[:].bitcast(FP8X4), lhsT_scale=w1_scales[:],
                                    rhs=picked_words[:, entries].bitcast(FP8X4), rhs_scale=picked_scales[:, entries],
                                    start=True, stop=True)
                to_relu.append((h[t][:, entries], bank))
        for rows, bank in to_relu:
            nc.scalar.activation(out=rows, in_=bank[:], func=ACT.Relu)

        w_words = keep.tile([P, 3, 2 * N], U8, name="w_words", tag="w1_raw1", align_bytes=64)
        for w in (NEAR, FAR, OWN):
            nc.scalar.copy(w_words[:, w, :].bitcast(U16).rearrange("p (t m) -> p t m", t=PACK),
                           w_words_raw[w][:].bitcast(U16).rearrange("p (m t) -> p t m", t=PACK))
        w_scales_dealt = keep.tile([P, N], U8, name="w_scales_dealt", tag="dealing", align_bytes=64)
        nc.vector.tensor_copy(w_scales_dealt[:].rearrange("p (t m) -> p t m", t=PACK),
                              w_scales_raw[:].rearrange("p (m t) -> p t m", t=PACK))
        for w in (NEAR, FAR, OWN):
            dealt_rows = w_scales_dealt[SCALE_ROWS * w : SCALE_ROWS * (w + 1), :]
            for q in range(QUADRANTS):
                rows, partitions = scale_rows(q)
                nc.sync.dma_start(w_scales[partitions, w, :].bitcast(I32), dealt_rows[rows, :].bitcast(I32))

        y_words = keep.tile([P, V], U32, name="y_words", align_bytes=64)
        y_scales = keep.tile([P, V], U8, name="y_scales", align_bytes=64)
        out_rows = out_0.rearrange("(p t) v -> p t v", t=PACK)
        own = keep.tile([P, PACK, V], BF16, name="own")

        def looked_up(t, entries, cols):
            return h[t][:].indirect(entries[:, cols.start // LIST_ROWS : cols.stop // LIST_ROWS])

        def fetch(out, t, entries, cols):
            nc.scalar.activation(out=out, in_=looked_up(t, entries, cols), func=ACT.Copy)

        def fetch_weighed(terms, lists, gates, t, d, cols):
            nc.vector.tensor_tensor(terms[:, t, d, cols], looked_up(t, lists[d], cols), gates[:, d, cols], ALU.mult)

        def weigh(terms, fetched, gates, t, first, cols):
            nc.vector.tensor_tensor(terms[:, t, first:, cols], fetched[:, t, first:, cols], gates[:, first:, cols], ALU.mult)

        def add_turned(total, terms, t, cols):
            for d in range(D):
                nc.tensor.matmul(total[:, t, :], lhsT=terms[:, t, d, cols], rhs=identity[:], is_transpose=True,
                                 start=(d == 0), stop=(d == D - 1))

        def turn_back(total):
            pairs = ring.tile([P, 2, P, 2], BF16, name="pairs", bufs=3)
            nc.scalar.activation(out=pairs[:], in_=total[:].rearrange("v (u e) p -> v u p e", e=2), func=ACT.Copy)
            words = pairs[:].rearrange("v u p e -> v u (p e)").bitcast(F32)
            back = turn.tile([P, 2, HALF], F32, name="back")
            for u in range(2):
                nc.tensor.transpose(back[:, u, :], words[:, u, :], identity[:])
            return back

        def woven_tile(name, bufs):
            return ring.tile([P, HALF * PACK], BF16, name=name, align_bytes=64, bufs=bufs)

        def by_runs(tiles):
            return tiles.rearrange("p t (c i) -> p c t i", i=RUN)

        def woven_by_runs(woven):
            return woven[:].rearrange("p (c i t) -> p c t i", i=RUN, t=PACK)

        def weave_back(back):
            z = woven_tile("z", PARTS)
            nc.scalar.copy(z[:].bitcast(F32).rearrange("p (v u) -> p v u", u=2), back[:].rearrange("p u v -> p v u"))
            return z

        def weave_own(cols):
            z = woven_tile("z", PARTS)
            nc.vector.tensor_copy(woven_by_runs(z), by_runs(own[:, :, cols]))
            return z

        def multiply(z, w, banks, opens=False, closes=False):
            z_codes = ring.tile([P, HALF], U32, name="z_codes", align_bytes=64, bufs=PARTS)
            z_scales = ring.tile([P, HALF], U8, name="z_scales", align_bytes=64, bufs=PARTS)
            nc.vector.quantize_mx(out=z_codes[:].bitcast(FP8X4), scales=z_scales[:], in_=z[:])
            for t in range(PACK):
                u, e = divmod(t, 2)
                nc.tensor.matmul_mx(out=banks[u][:, e, :], lhsT=w_words[:, w, 2 * P * t : 2 * P * (t + 1)].bitcast(FP4X4),
                                    lhsT_scale=w_scales[:, w, P * t : P * (t + 1)],
                                    rhs=z_codes[:].bitcast(FP8X4), rhs_scale=z_scales[:],
                                    start=(opens and e == 0), stop=(closes and e == 1))

        def quantise_y(y_bf, cols):
            nc.vector.quantize_mx(out=y_words[:, cols].bitcast(FP8X4), scales=y_scales[:, cols], in_=y_bf[:])

        fetched_near = ring.tile([P, PACK, D, V], F32, name="fetched")
        fetch(fetched_near[:, PACK - 1, D - 1, :], PACK - 1, near[D - 1], BOTH)
        terms_near = ring.tile([P, PACK, D, V], F32, name="terms")
        for t in range(PACK):
            for d in range(D if t < PACK - 1 else D - 1):
                fetch_weighed(terms_near, near, gate_near, t, d, BOTH)
        weigh(terms_near, fetched_near, gate_near, PACK - 1, D - 1, BOTH)
        near_first, near_last = [acc.tile([P, PACK, P], F32, name="bank%d" % u) for u in range(2)]
        for t in range(PACK):
            add_turned(near_first, terms_near, t, FIRST)
            add_turned(near_last, terms_near, t, LAST)

        far_first_on_scalar = D - FAR_ON_SCALAR
        fetched_far = ring.tile([P, PACK, D, V], F32, name="fetched")
        for t in range(PACK):
            for d in range(far_first_on_scalar, D):
                fetch(fetched_far[:, t, d, :], t, far[d], BOTH)
        terms_far = ring.tile([P, PACK, D, V], F32, name="terms")
        banks_first = [acc.tile([P, 2, HALF], F32, name="bank%d" % (2 + u)) for u in range(2)]
        banks_last = [acc.tile([P, 2, HALF], F32, name="bank%d" % u) for u in range(2)]
        for t in range(PACK):
            fetch(own[:, t, FIRST], t, cen_list, FIRST)
        back_first = turn_back(near_first)
        back_last = turn_back(near_last)
        multiply(weave_back(back_first), NEAR, banks_first, opens=True)
        multiply(weave_back(back_last), NEAR, banks_last, opens=True)

        for t in range(PACK):
            for d in range(far_first_on_scalar):
                fetch_weighed(terms_far, far, gate_far, t, d, FIRST)
            weigh(terms_far, fetched_far, gate_far, t, far_first_on_scalar, FIRST)
        far_first = turn.tile([P, PACK, P], F32, name="far_first", bufs=1)
        for t in range(PACK):
            add_turned(far_first, terms_far, t, FIRST)
        z2_first = weave_back(turn_back(far_first))
        for t in range(PACK):
            fetch(own[:, t, LAST], t, cen_list, LAST)

        two_terms = ring.tile([P, PACK, HALF], F32, name="two_terms")
        for t in range(PACK):
            weigh(terms_far, fetched_far, gate_far, t, far_first_on_scalar, LAST)
        for t in range(PACK):
            fetch_weighed(terms_far, far, gate_far, t, 0, LAST)
            if t == 0:
                nc.vector.tensor_tensor(two_terms[:], terms_far[:, :, 1, LAST], terms_far[:, :, 2, LAST], ALU.add)
        multiply(weave_own(FIRST), OWN, banks_first)
        multiply(z2_first, FAR, banks_first, closes=True)
        z2_last = woven_tile("z", PARTS)
        nc.vector.tensor_tensor(woven_by_runs(z2_last), by_runs(terms_far[:, :, 0, LAST]), by_runs(two_terms[:]), ALU.add)
        multiply(weave_own(LAST), OWN, banks_last)
        multiply(z2_last, FAR, banks_last, closes=True)

        y_first = ring.tile([P, PACK, HALF], F32, name="y")
        for u in range(2):
            nc.scalar.copy(y_first[:, 2 * u : 2 * u + 2, :], banks_first[u][:])
        nc.sync.dma_start(out_rows[:, :, FIRST], y_first[:])
        y_first_bf = woven_tile("y_bf", 2)
        nc.vector.tensor_copy(woven_by_runs(y_first_bf), by_runs(y_first[:]))
        quantise_y(y_first_bf, FIRST)

        y_last_bf = woven_tile("y_bf", 2)
        y_pairs = y_last_bf[:].rearrange("p (v u e) -> p u v e", u=2, e=2)
        y_last = ring.tile([P, PACK, HALF], F32, name="y")
        copies = (nc.scalar.copy, nc.vector.tensor_copy)
        for u in range(2):
            copies[u](y_pairs[:, u], banks_last[u][:].rearrange("p e v -> p v e"))
        for u in range(2):
            copies[u](y_last[:, 2 * u : 2 * u + 2, :], banks_last[u][:])
        for u, queue in enumerate((nc.scalar, nc.sync)):
            queue.dma_start(out_rows[:, 2 * u : 2 * u + 2, LAST], y_last[:, 2 * u : 2 * u + 2, :])
        quantise_y(y_last_bf, LAST)

        nc.scalar.dma_start(out_1[0].rearrange("p v t -> p (v t)").bitcast(I32), y_words[:].bitcast(I32))
        for q in range(QUADRANTS):
            rows, partitions = scale_rows(q)
            queue = nc.sync if q < QUADRANTS - 1 else nc.scalar
            queue.dma_start(out_2[0, rows, :].bitcast(I32), y_scales[partitions, :].bitcast(I32))
